import numpy as np
import ml_dtypes

BF16 = ml_dtypes.bfloat16


def bf(x):
    return np.asarray(x, np.float32).astype(BF16)


def f32(x):
    return np.asarray(x, np.float32)


def f64(x):
    return np.asarray(x).astype(np.float64)


def striped(idx):
    return np.tile(idx.reshape(-1, 16).T, (8, 1))


def rows(idx, k):
    return np.tile(idx, (k, 1))


def look(tab, idx):
    return np.take_along_axis(f64(tab), rows(idx, len(tab)), axis=1)


K, S, D, V, N, M = 256, 4096, 2, 2048, 4096, 256


def setup_inputs():
    return {"tab": f32(np.random.standard_normal((K, S))), "x0": f32(np.random.standard_normal((K, V))), "w": bf(np.random.standard_normal((K, M)) / np.sqrt(K)), "b": f32(0.5 * np.random.standard_normal((M, 1))), "offs": striped(np.random.permutation(S)[:N])}


def reference(tab, x0, w, b, offs):
    idx = offs[:16].T.reshape(-1)
    x = f64(x0)
    for d in range(D):
        x = np.maximum(x, look(tab, idx[d * V:(d + 1) * V]))
    y = f64(w).T @ x
    return np.maximum(y + f64(b), 0.0)

@@ -1,0 +1,68 @@
+import concourse.mybir as mybir
+
+P = 128
+K, S, V, M = 256, 4096, 2048, 256
+LANES = 16
+WIDTH = 512
+
+FLOPS = 2 * K * M * V
+
+BF16, F32, U16 = mybir.dt.bfloat16, mybir.dt.float32, mybir.dt.uint16
+
+
+def tile_lookup_pool_max_relu_kernel(tc, tab, x0, w, b, offs, out):
+    nc = tc.nc
+    largest = mybir.AluOpType.max
+    relu = mybir.ActivationFunctionType.Relu
+    blocks = K // P
+    halves = M // P
+    starts = range(0, V, WIDTH)
+    out_rows = out.rearrange("(p h) j -> p h j", h=halves)
+
+    with (
+        tc.tile_pool(name="held", bufs=1) as held,
+        tc.psum_pool(name="psum", bufs=4) as psum,
+    ):
+        offsets = held.tile([P, 2 * V // LANES], U16, name="offsets")
+        nc.sync.dma_start(offsets[:], offs)
+
+        table, centre = [], []
+        for k in range(blocks):
+            rows = slice(k * P, (k + 1) * P)
+            table.append(held.tile([P, S], F32, name=f"table{k}"))
+            centre.append(held.tile([P, V], F32, name=f"centre{k}"))
+            nc.sync.dma_start(table[k][:], tab[rows, :])
+            for c in starts:
+                nc.sync.dma_start(centre[k][:, c : c + WIDTH], x0[rows, c : c + WIDTH])
+
+        weights = held.tile([P, blocks, M], BF16, name="weights")
+        nc.sync.dma_start(weights[:], w.rearrange("(k p) m -> p k m", p=P))
+        bias = held.tile([P, halves], F32, name="bias")
+        nc.sync.dma_start(bias[:], b.rearrange("(p h) o -> p (h o)", h=halves))
+
+        def neighbours(k, d, c):
+            first = (d * V + c) // LANES
+            return table[k][:].indirect(offsets[:, first : first + WIDTH // LANES])
+
+        pooled = []
+        for k in range(blocks):
+            partial = held.tile([P, V], F32, name=f"partial{k}")
+            exact = held.tile([P, V], F32, name=f"exact{k}")
+            pooled.append(held.tile([P, V], BF16, name=f"pooled{k}"))
+            for c in starts:
+                cols = slice(c, c + WIDTH)
+                nc.vector.tensor_tensor(partial[:, cols], neighbours(k, 0, c), centre[k][:, cols], largest)
+                nc.vector.tensor_tensor(exact[:, cols], neighbours(k, 1, c), partial[:, cols], largest)
+                nc.scalar.copy(pooled[k][:, cols], exact[:, cols])
+
+        for c in starts:
+            cols = slice(c, c + WIDTH)
+            result = held.tile([P, halves, WIDTH], F32, name=f"result{c}")
+            for h in range(halves):
+                product = psum.tile([P, WIDTH], F32, name=f"product{h}")
+                for k in range(blocks):
+                    nc.tensor.matmul(
+                        product[:], weights[:, k, h::halves], pooled[k][:, cols], start=k == 0, stop=k == blocks - 1
+                    )
+                nc.scalar.activation(result[:, h, :], product[:], relu, bias=bias[:, h : h + 1])
+            nc.sync.dma_start(out_rows[:, :, cols], result[:])

@@ -3,7 +3,8 @@ import concourse.mybir as mybir
 P = 128
 K, S, V, M = 256, 4096, 2048, 256
 LANES = 16
-WIDTH = 512
+EARLY = (256,) * 6
+LATE = (256, 128, 128)
 
 FLOPS = 2 * K * M * V
 
@@ -12,11 +13,15 @@ BF16, F32, U16 = mybir.dt.bfloat16, mybir.dt.float32, mybir.dt.uint16
 
 def tile_lookup_pool_max_relu_kernel(tc, tab, x0, w, b, offs, out):
     nc = tc.nc
-    largest = mybir.AluOpType.max
+    largest, add = mybir.AluOpType.max, mybir.AluOpType.add
     relu = mybir.ActivationFunctionType.Relu
     blocks = K // P
     halves = M // P
-    starts = range(0, V, WIDTH)
+    widths = EARLY + LATE
+    edges = [sum(widths[:i]) for i in range(len(widths) + 1)]
+    pieces = [slice(lo, hi) for lo, hi in zip(edges, edges[1:])]
+    early, late = pieces[: len(EARLY)], pieces[len(EARLY) :]
+    units = [(k, cols) for k in range(blocks) for cols in early] + [(k, cols) for cols in late for k in range(blocks)]
     out_rows = out.rearrange("(p h) j -> p h j", h=halves)
 
     with (
@@ -24,45 +29,64 @@ def tile_lookup_pool_max_relu_kernel(tc, tab, x0, w, b, offs, out):
         tc.psum_pool(name="psum", bufs=4) as psum,
     ):
         offsets = held.tile([P, 2 * V // LANES], U16, name="offsets")
-        nc.sync.dma_start(offsets[:], offs)
+        table = [held.tile([P, S], F32, name=f"table{k}") for k in range(blocks)]
+        centre = [held.tile([P, V], F32, name=f"centre{k}") for k in range(blocks)]
+        partial = [held.tile([P, V], F32, name=f"partial{k}") for k in range(blocks)]
+        exact = [held.tile([P, V], F32, name=f"exact{k}") for k in range(blocks)]
+        rounded = [held.tile([P, V], BF16, name=f"rounded{k}") for k in range(blocks)]
+        result = held.tile([P, halves, V], F32, name="result")
+        weights = held.tile([P, blocks, M], BF16, name="weights")
+        bias = held.tile([P, halves], F32, name="bias")
 
-        table, centre = [], []
+        nc.sync.dma_start(offsets[:], offs)
         for k in range(blocks):
             rows = slice(k * P, (k + 1) * P)
-            table.append(held.tile([P, S], F32, name=f"table{k}"))
-            centre.append(held.tile([P, V], F32, name=f"centre{k}"))
             nc.sync.dma_start(table[k][:], tab[rows, :])
-            for c in starts:
-                nc.sync.dma_start(centre[k][:, c : c + WIDTH], x0[rows, c : c + WIDTH])
-
-        weights = held.tile([P, blocks, M], BF16, name="weights")
+            for cols in early:
+                nc.sync.dma_start(centre[k][:, cols], x0[rows, cols])
         nc.sync.dma_start(weights[:], w.rearrange("(k p) m -> p k m", p=P))
-        bias = held.tile([P, halves], F32, name="bias")
         nc.sync.dma_start(bias[:], b.rearrange("(p h) o -> p (h o)", h=halves))
-
-        def neighbours(k, d, c):
-            first = (d * V + c) // LANES
-            return table[k][:].indirect(offsets[:, first : first + WIDTH // LANES])
-
-        pooled = []
         for k in range(blocks):
-            partial = held.tile([P, V], F32, name=f"partial{k}")
-            exact = held.tile([P, V], F32, name=f"exact{k}")
-            pooled.append(held.tile([P, V], BF16, name=f"pooled{k}"))
-            for c in starts:
-                cols = slice(c, c + WIDTH)
-                nc.vector.tensor_tensor(partial[:, cols], neighbours(k, 0, c), centre[k][:, cols], largest)
-                nc.vector.tensor_tensor(exact[:, cols], neighbours(k, 1, c), partial[:, cols], largest)
-                nc.scalar.copy(pooled[k][:, cols], exact[:, cols])
+            nc.sync.dma_start(centre[k][:, late[0].start :], x0[k * P : (k + 1) * P, late[0].start :])
 
-        for c in starts:
-            cols = slice(c, c + WIDTH)
-            result = held.tile([P, halves, WIDTH], F32, name=f"result{c}")
-            for h in range(halves):
-                product = psum.tile([P, WIDTH], F32, name=f"product{h}")
-                for k in range(blocks):
+        def neighbours(k, d, cols):
+            entries = offsets[:, (d * V + cols.start) // LANES : (d * V + cols.stop) // LANES]
+            return table[k][:].indirect(entries)
+
+        products = {}
+
+        def multiply(cols):
+            width = cols.stop - cols.start
+            products[cols.start] = [psum.tile([P, width], F32, name=f"product{h}") for h in range(halves)]
+            for k in range(blocks):
+                for h, product in enumerate(products[cols.start]):
                     nc.tensor.matmul(
-                        product[:], weights[:, k, h::halves], pooled[k][:, cols], start=k == 0, stop=k == blocks - 1
+                        product[:], weights[:, k, h::halves], rounded[k][:, cols], start=k == 0, stop=k == blocks - 1
                     )
-                nc.scalar.activation(result[:, h, :], product[:], relu, bias=bias[:, h : h + 1])
-            nc.sync.dma_start(out_rows[:, :, cols], result[:])
+
+        def finish(cols):
+            for h, product in enumerate(products[cols.start]):
+                if cols == pieces[-1] and h > 0:
+                    nc.vector.tensor_scalar(result[:, h, cols], product[:], bias[:, h : h + 1], 0.0, add, largest)
+                else:
+                    nc.scalar.activation(result[:, h, cols], product[:], relu, bias=bias[:, h : h + 1])
+            nc.sync.dma_start(out_rows[:, :, cols], result[:, :, cols])
+
+        multiplied = []
+        for pair in zip(units[::2], units[1::2]):
+            for k, cols in pair:
+                nc.vector.tensor_tensor(partial[k][:, cols], neighbours(k, 0, cols), centre[k][:, cols], largest)
+            waiting, multiplied = multiplied, []
+            for k, cols in pair:
+                nc.vector.tensor_tensor(exact[k][:, cols], neighbours(k, 1, cols), partial[k][:, cols], largest)
+                if (k, cols) == units[-1]:
+                    nc.vector.tensor_copy(rounded[k][:, cols], exact[k][:, cols])
+                else:
+                    nc.scalar.copy(rounded[k][:, cols], exact[k][:, cols])
+                if k == blocks - 1:
+                    multiply(cols)
+                    multiplied.append(cols)
+            for cols in waiting:
+                finish(cols)
+        for cols in multiplied:
+            finish(cols)

@@ -3,6 +3,7 @@ import concourse.mybir as mybir
 P = 128
 K, S, V, M = 256, 4096, 2048, 256
 LANES = 16
+LEAD = (256, 256, 512, 512)
 EARLY = (256,) * 6
 LATE = (256, 128, 128)
 
@@ -11,17 +12,20 @@ FLOPS = 2 * K * M * V
 BF16, F32, U16 = mybir.dt.bfloat16, mybir.dt.float32, mybir.dt.uint16
 
 
+def cut(widths):
+    return [slice(sum(widths[:i]), sum(widths[: i + 1])) for i in range(len(widths))]
+
+
 def tile_lookup_pool_max_relu_kernel(tc, tab, x0, w, b, offs, out):
     nc = tc.nc
-    largest, add = mybir.AluOpType.max, mybir.AluOpType.add
+    largest = mybir.AluOpType.max
     relu = mybir.ActivationFunctionType.Relu
     blocks = K // P
     halves = M // P
-    widths = EARLY + LATE
-    edges = [sum(widths[:i]) for i in range(len(widths) + 1)]
-    pieces = [slice(lo, hi) for lo, hi in zip(edges, edges[1:])]
-    early, late = pieces[: len(EARLY)], pieces[len(EARLY) :]
-    units = [(k, cols) for k in range(blocks) for cols in early] + [(k, cols) for cols in late for k in range(blocks)]
+    pieces = cut(EARLY + LATE)
+    lead, early, late = cut(LEAD), pieces[: len(EARLY)], pieces[len(EARLY) :]
+    units = [(0, cols) for cols in lead] + [(1, cols) for cols in early]
+    units += [(k, cols) for cols in late for k in range(blocks)]
     out_rows = out.rearrange("(p h) j -> p h j", h=halves)
 
     with (
@@ -31,10 +35,10 @@ def tile_lookup_pool_max_relu_kernel(tc, tab, x0, w, b, offs, out):
         offsets = held.tile([P, 2 * V // LANES], U16, name="offsets")
         table = [held.tile([P, S], F32, name=f"table{k}") for k in range(blocks)]
         centre = [held.tile([P, V], F32, name=f"centre{k}") for k in range(blocks)]
-        partial = [held.tile([P, V], F32, name=f"partial{k}") for k in range(blocks)]
+        widest = max(LEAD)
+        partial = [held.tile([P, widest], F32, name=f"partial{i}") for i in range(4)]
         exact = [held.tile([P, V], F32, name=f"exact{k}") for k in range(blocks)]
         rounded = [held.tile([P, V], BF16, name=f"rounded{k}") for k in range(blocks)]
-        result = held.tile([P, halves, V], F32, name="result")
         weights = held.tile([P, blocks, M], BF16, name="weights")
         bias = held.tile([P, halves], F32, name="bias")
 
@@ -42,10 +46,12 @@ def tile_lookup_pool_max_relu_kernel(tc, tab, x0, w, b, offs, out):
         for k in range(blocks):
             rows = slice(k * P, (k + 1) * P)
             nc.sync.dma_start(table[k][:], tab[rows, :])
-            for cols in early:
+            if k == blocks - 1:
+                nc.sync.dma_start(bias[:], b.rearrange("(p h) o -> p (h o)", h=halves))
+            for cols in lead:
                 nc.sync.dma_start(centre[k][:, cols], x0[rows, cols])
-        nc.sync.dma_start(weights[:], w.rearrange("(k p) m -> p k m", p=P))
-        nc.sync.dma_start(bias[:], b.rearrange("(p h) o -> p (h o)", h=halves))
+            if k == 0:
+                nc.sync.dma_start(weights[:], w.rearrange("(k p) m -> p k m", p=P))
         for k in range(blocks):
             nc.sync.dma_start(centre[k][:, late[0].start :], x0[k * P : (k + 1) * P, late[0].start :])
 
@@ -65,28 +71,26 @@ def tile_lookup_pool_max_relu_kernel(tc, tab, x0, w, b, offs, out):
                     )
 
         def finish(cols):
+            result = held.tile([P, halves, cols.stop - cols.start], F32, name=f"result{cols.start}")
             for h, product in enumerate(products[cols.start]):
-                if cols == pieces[-1] and h > 0:
-                    nc.vector.tensor_scalar(result[:, h, cols], product[:], bias[:, h : h + 1], 0.0, add, largest)
-                else:
-                    nc.scalar.activation(result[:, h, cols], product[:], relu, bias=bias[:, h : h + 1])
-            nc.sync.dma_start(out_rows[:, :, cols], result[:, :, cols])
+                nc.scalar.activation(result[:, h, :], product[:], relu, bias=bias[:, h : h + 1])
+            nc.sync.dma_start(out_rows[:, :, cols], result[:])
 
-        multiplied = []
-        for pair in zip(units[::2], units[1::2]):
-            for k, cols in pair:
-                nc.vector.tensor_tensor(partial[k][:, cols], neighbours(k, 0, cols), centre[k][:, cols], largest)
-            waiting, multiplied = multiplied, []
-            for k, cols in pair:
-                nc.vector.tensor_tensor(exact[k][:, cols], neighbours(k, 1, cols), partial[k][:, cols], largest)
-                if (k, cols) == units[-1]:
-                    nc.vector.tensor_copy(rounded[k][:, cols], exact[k][:, cols])
-                else:
-                    nc.scalar.copy(rounded[k][:, cols], exact[k][:, cols])
+        waiting = []
+        for first in range(0, len(units), 2):
+            pair = list(enumerate(units))[first : first + 2]
+            for u, (k, cols) in pair:
+                so_far = partial[u % len(partial)][:, : cols.stop - cols.start]
+                nc.vector.tensor_tensor(so_far, neighbours(k, 0, cols), centre[k][:, cols], largest)
+            for u, (k, cols) in pair:
+                so_far = partial[u % len(partial)][:, : cols.stop - cols.start]
+                pooled = exact[k][:, cols]
+                nc.vector.tensor_tensor(pooled, neighbours(k, 1, cols), so_far, largest)
+                nc.scalar.copy(rounded[k][:, cols], pooled)
                 if k == blocks - 1:
                     multiply(cols)
-                    multiplied.append(cols)
             for cols in waiting:
                 finish(cols)
-        for cols in multiplied:
+            waiting = [cols for u, (k, cols) in pair if k == blocks - 1]
+        for cols in waiting:
             finish(cols)

@@ -3,9 +3,10 @@ import concourse.mybir as mybir
 P = 128
 K, S, V, M = 256, 4096, 2048, 256
 LANES = 16
-LEAD = (256, 256, 512, 512)
+LEAD = (192, 192, 576, 576)
 EARLY = (256,) * 6
 LATE = (256, 128, 128)
+LAG = 2
 
 FLOPS = 2 * K * M * V
 
@@ -18,7 +19,7 @@ def cut(widths):
 
 def tile_lookup_pool_max_relu_kernel(tc, tab, x0, w, b, offs, out):
     nc = tc.nc
-    largest = mybir.AluOpType.max
+    largest, add = mybir.AluOpType.max, mybir.AluOpType.add
     relu = mybir.ActivationFunctionType.Relu
     blocks = K // P
     halves = M // P
@@ -42,16 +43,17 @@ def tile_lookup_pool_max_relu_kernel(tc, tab, x0, w, b, offs, out):
         weights = held.tile([P, blocks, M], BF16, name="weights")
         bias = held.tile([P, halves], F32, name="bias")
 
-        nc.sync.dma_start(offsets[:], offs)
-        for k in range(blocks):
+        for k, group in enumerate((lead, early)):
             rows = slice(k * P, (k + 1) * P)
             nc.sync.dma_start(table[k][:], tab[rows, :])
-            if k == blocks - 1:
-                nc.sync.dma_start(bias[:], b.rearrange("(p h) o -> p (h o)", h=halves))
-            for cols in lead:
-                nc.sync.dma_start(centre[k][:, cols], x0[rows, cols])
             if k == 0:
-                nc.sync.dma_start(weights[:], w.rearrange("(k p) m -> p k m", p=P))
+                nc.sync.dma_start(offsets[:], offs)
+            for left, right in zip(group[::2], group[1::2]):
+                cols = slice(left.start, right.stop)
+                nc.sync.dma_start(centre[k][:, cols], x0[rows, cols])
+                if k == blocks - 1 and cols.start == 0:
+                    nc.sync.dma_start(weights[:], w.rearrange("(k p) m -> p k m", p=P))
+                    nc.sync.dma_start(bias[:], b.rearrange("(p h) o -> p (h o)", h=halves))
         for k in range(blocks):
             nc.sync.dma_start(centre[k][:, late[0].start :], x0[k * P : (k + 1) * P, late[0].start :])
 
@@ -73,24 +75,27 @@ def tile_lookup_pool_max_relu_kernel(tc, tab, x0, w, b, offs, out):
         def finish(cols):
             result = held.tile([P, halves, cols.stop - cols.start], F32, name=f"result{cols.start}")
             for h, product in enumerate(products[cols.start]):
-                nc.scalar.activation(result[:, h, :], product[:], relu, bias=bias[:, h : h + 1])
+                if cols == pieces[-1] and h > 0:
+                    nc.vector.tensor_scalar(result[:, h, :], product[:], bias[:, h : h + 1], 0.0, add, largest)
+                else:
+                    nc.scalar.activation(result[:, h, :], product[:], relu, bias=bias[:, h : h + 1])
             nc.sync.dma_start(out_rows[:, :, cols], result[:])
 
-        waiting = []
         for first in range(0, len(units), 2):
-            pair = list(enumerate(units))[first : first + 2]
-            for u, (k, cols) in pair:
+            pair = range(first, first + 2)
+            for u in pair:
+                k, cols = units[u]
                 so_far = partial[u % len(partial)][:, : cols.stop - cols.start]
                 nc.vector.tensor_tensor(so_far, neighbours(k, 0, cols), centre[k][:, cols], largest)
-            for u, (k, cols) in pair:
+            for u in pair:
+                k, cols = units[u]
                 so_far = partial[u % len(partial)][:, : cols.stop - cols.start]
-                pooled = exact[k][:, cols]
-                nc.vector.tensor_tensor(pooled, neighbours(k, 1, cols), so_far, largest)
-                nc.scalar.copy(rounded[k][:, cols], pooled)
+                nc.vector.tensor_tensor(exact[k][:, cols], neighbours(k, 1, cols), so_far, largest)
+                nc.scalar.copy(rounded[k][:, cols], exact[k][:, cols])
                 if k == blocks - 1:
                     multiply(cols)
-            for cols in waiting:
+                if u >= LAG and units[u - LAG][0] == blocks - 1:
+                    finish(units[u - LAG][1])
+        for k, cols in units[-LAG:]:
+            if k == blocks - 1:
                 finish(cols)
-            waiting = [cols for u, (k, cols) in pair if k == blocks - 1]
-        for cols in waiting:
-            finish(cols)

import concourse.mybir as mybir

P = 128
K, S, V, M = 256, 4096, 2048, 256
LANES = 16
LEAD = (192, 192, 576, 576)
EARLY = (256,) * 6
LATE = (256, 128, 128)
LAG = 2

FLOPS = 2 * K * M * V

BF16, F32, U16 = mybir.dt.bfloat16, mybir.dt.float32, mybir.dt.uint16


def cut(widths):
    return [slice(sum(widths[:i]), sum(widths[: i + 1])) for i in range(len(widths))]


def tile_lookup_pool_max_relu_kernel(tc, tab, x0, w, b, offs, out):
    nc = tc.nc
    largest, add = mybir.AluOpType.max, mybir.AluOpType.add
    relu = mybir.ActivationFunctionType.Relu
    blocks = K // P
    halves = M // P
    pieces = cut(EARLY + LATE)
    lead, early, late = cut(LEAD), pieces[: len(EARLY)], pieces[len(EARLY) :]
    units = [(0, cols) for cols in lead] + [(1, cols) for cols in early]
    units += [(k, cols) for cols in late for k in range(blocks)]
    out_rows = out.rearrange("(p h) j -> p h j", h=halves)

    with (
        tc.tile_pool(name="held", bufs=1) as held,
        tc.psum_pool(name="psum", bufs=4) as psum,
    ):
        offsets = held.tile([P, 2 * V // LANES], U16, name="offsets")
        table = [held.tile([P, S], F32, name=f"table{k}") for k in range(blocks)]
        centre = [held.tile([P, V], F32, name=f"centre{k}") for k in range(blocks)]
        widest = max(LEAD)
        partial = [held.tile([P, widest], F32, name=f"partial{i}") for i in range(4)]
        exact = [held.tile([P, V], F32, name=f"exact{k}") for k in range(blocks)]
        rounded = [held.tile([P, V], BF16, name=f"rounded{k}") for k in range(blocks)]
        weights = held.tile([P, blocks, M], BF16, name="weights")
        bias = held.tile([P, halves], F32, name="bias")

        for k, group in enumerate((lead, early)):
            rows = slice(k * P, (k + 1) * P)
            nc.sync.dma_start(table[k][:], tab[rows, :])
            if k == 0:
                nc.sync.dma_start(offsets[:], offs)
            for left, right in zip(group[::2], group[1::2]):
                cols = slice(left.start, right.stop)
                nc.sync.dma_start(centre[k][:, cols], x0[rows, cols])
                if k == blocks - 1 and cols.start == 0:
                    nc.sync.dma_start(weights[:], w.rearrange("(k p) m -> p k m", p=P))
                    nc.sync.dma_start(bias[:], b.rearrange("(p h) o -> p (h o)", h=halves))
        for k in range(blocks):
            nc.sync.dma_start(centre[k][:, late[0].start :], x0[k * P : (k + 1) * P, late[0].start :])

        def neighbours(k, d, cols):
            entries = offsets[:, (d * V + cols.start) // LANES : (d * V + cols.stop) // LANES]
            return table[k][:].indirect(entries)

        products = {}

        def multiply(cols):
            width = cols.stop - cols.start
            products[cols.start] = [psum.tile([P, width], F32, name=f"product{h}") for h in range(halves)]
            for k in range(blocks):
                for h, product in enumerate(products[cols.start]):
                    nc.tensor.matmul(
                        product[:], weights[:, k, h::halves], rounded[k][:, cols], start=k == 0, stop=k == blocks - 1
                    )

        def finish(cols):
            result = held.tile([P, halves, cols.stop - cols.start], F32, name=f"result{cols.start}")
            for h, product in enumerate(products[cols.start]):
                if cols == pieces[-1] and h > 0:
                    nc.vector.tensor_scalar(result[:, h, :], product[:], bias[:, h : h + 1], 0.0, add, largest)
                else:
                    nc.scalar.activation(result[:, h, :], product[:], relu, bias=bias[:, h : h + 1])
            nc.sync.dma_start(out_rows[:, :, cols], result[:])

        for first in range(0, len(units), 2):
            pair = range(first, first + 2)
            for u in pair:
                k, cols = units[u]
                so_far = partial[u % len(partial)][:, : cols.stop - cols.start]
                nc.vector.tensor_tensor(so_far, neighbours(k, 0, cols), centre[k][:, cols], largest)
            for u in pair:
                k, cols = units[u]
                so_far = partial[u % len(partial)][:, : cols.stop - cols.start]
                nc.vector.tensor_tensor(exact[k][:, cols], neighbours(k, 1, cols), so_far, largest)
                nc.scalar.copy(rounded[k][:, cols], exact[k][:, cols])
                if k == blocks - 1:
                    multiply(cols)
                if u >= LAG and units[u - LAG][0] == blocks - 1:
                    finish(units[u - LAG][1])
        for k, cols in units[-LAG:]:
            if k == blocks - 1:
                finish(cols)
